import numpy as np
import ml_dtypes


def mxq(x, axis, fmt="e4m3"):
    dtype, down = {"e4m3": (ml_dtypes.float8_e4m3fn, 7), "e5m2": (ml_dtypes.float8_e5m2, 14)}[fmt]
    v = np.moveaxis(np.asarray(x, np.float32).astype(ml_dtypes.bfloat16).astype(np.float64), axis, -1)
    blocks = v.reshape(v.shape[:-1] + (-1, 32))
    amax = np.abs(blocks).max(-1, keepdims=True)
    byte = np.maximum(np.where(amax > 0, np.frexp(amax)[1] - 1 + 127, 0) - down, 1)
    scale = np.exp2(byte - 127.0)
    codes = (blocks / scale).astype(np.float32).astype(dtype).astype(np.float64)
    return np.moveaxis((codes * scale).reshape(v.shape), -1, axis)


WIDE = False


def mx_kscale(k):
    if not WIDE:
        return np.ones(k)
    levels = np.array([10, -10, 5, -5, 0])
    if k % 512:
        return np.exp2(np.random.permutation(np.resize(levels, k // 32))).repeat(32)
    a = np.empty((k // 512, 16))
    for p in range(k // 512):
        a[p, :8] = np.random.permutation(np.resize(levels, 8))
        for g in range(8):
            far = levels[np.abs(levels - a[p, g]) >= 10]
            a[p, g + 8] = far[np.random.randint(len(far))]
    return np.exp2(a.ravel()).repeat(32)


BF16 = ml_dtypes.bfloat16


def bf(x):
    return np.asarray(x, np.float32).astype(BF16)


def f64(x):
    return np.asarray(x).astype(np.float64)


E2M1 = np.array([0.0, 0.5, 1.0, 1.5, 2.0, 3.0, 4.0, 6.0, -0.0, -0.5, -1.0, -1.5, -2.0, -3.0, -4.0, -6.0])


def pack_weight(w, fmt):
    k, n = w.shape
    w = f64(bf(w)).reshape(k // 32, 32, n)
    amax = np.abs(w).max(1)
    if fmt == "e4m3":
        byte = np.frexp(amax)[1] - 1 + 127 - 7
    else:
        mant, ex = np.frexp(amax / 6.0)
        byte = np.where(mant > 0.5, ex, ex - 1) + 127
    byte = np.clip(np.where(amax > 0, byte, 1), 1, 254)
    scaled = (w * np.exp2(127.0 - byte)[:, None, :]).reshape(k, n).astype(np.float32)
    by_word = np.ascontiguousarray(scaled.reshape(k // 512, 128, 4, n).transpose(0, 1, 3, 2))
    if fmt == "e4m3":
        words = by_word.astype(ml_dtypes.float8_e4m3fn).view(np.uint8)
    else:
        c = by_word.astype(ml_dtypes.float4_e2m1fn).view(np.uint8) & 0xF
        words = c[..., 0::2] | (c[..., 1::2] << 4)
    return np.ascontiguousarray(words), np.ascontiguousarray(byte.astype(np.uint8).reshape(k // 512, 16, n))


def unpack_weight(words, scales, fmt):
    g, p, n, _ = words.shape
    if fmt == "e4m3":
        vals = np.ascontiguousarray(words).view(ml_dtypes.float8_e4m3fn).astype(np.float64)
    else:
        nib = np.empty((g, p, n, 4), np.uint8)
        nib[..., 0::2] = words & 0xF
        nib[..., 1::2] = words >> 4
        vals = E2M1[nib]
    vals = vals * np.repeat(np.exp2(scales.astype(np.float64) - 127.0), 8, axis=1)[..., None]
    return vals.transpose(0, 1, 3, 2).reshape(g * 512, n)
def pack4(w):
    words, scales = pack_weight(w, "e2m1")
    return words.reshape(words.shape[0], 128, -1), scales


def unpack4(words, scales):
    return unpack_weight(words.reshape(words.shape[0], 128, -1, 2), scales, "e2m1")


M, R, B = 2048, 1024, 512

E_MIN = 0.5


def draw0():
    s, t = mx_kscale(R), mx_kscale(M)
    phi = np.random.standard_normal((M, R)) * s * t[:, None]
    coef = np.random.standard_normal((R, B)) / np.sqrt(R) / s[:, None]
    energy = np.sqrt(E_MIN ** 2 + np.random.standard_normal((M, B)) ** 2)
    v = np.random.standard_normal((M, M)) / np.sqrt(M) / t[:, None]
    v_words, v_scales = pack4(v)
    return {"phi": bf(phi),
            "coef": bf(coef),
            "energy": bf(energy),
            "v_words": v_words,
            "v_scales": v_scales}


def core(phi, coef, energy, v_words, v_scales):
    gap = mxq(f64(phi), 1, "e4m3") @ mxq(f64(coef), 0, "e4m3")
    e = f64(energy)
    h = gap * np.tanh(e) / e
    v = unpack4(v_words, v_scales)
    return v.T @ mxq(h, 0, "e4m3")


def e4m3fn_bytes(y):
    return np.clip(np.asarray(y, np.float64), -448.0, 448.0).astype(np.float32).astype(ml_dtypes.float8_e4m3fn).view(np.uint8)


def e4m3fn_values(b):
    return np.asarray(b, np.uint8).view(ml_dtypes.float8_e4m3fn).astype(np.float64)


def setup_inputs():
    d = draw0()
    x0 = np.asarray(d['coef']).astype(np.float64)
    s = (np.max(np.abs(x0), axis=(1,), keepdims=True) / 448.0).astype(np.float32)
    out = {}
    for k, v in d.items():
        if k == 'coef':
            out['coef_bytes'] = e4m3fn_bytes(x0 / s.astype(np.float64))
            out['coef_scale'] = s
        else:
            out[k] = v
    return out


def reference(phi, coef_bytes, coef_scale, energy, v_words, v_scales):
    return core(phi, e4m3fn_values(coef_bytes) * coef_scale.astype(np.float64), energy, v_words, v_scales)

@@ -1,0 +1,424 @@
+from contextlib import ExitStack
+
+import concourse.mybir as mybir
+from concourse.masks import make_identity
+
+M, R, B = 2048, 1024, 512
+FLOPS = 2 * M * R * B + 2 * M * M * B
+
+F32 = mybir.dt.float32
+BF16 = mybir.dt.bfloat16
+U32 = mybir.dt.uint32
+I32 = mybir.dt.int32
+U8 = mybir.dt.uint8
+FP8 = mybir.dt.float8_e4m3fn
+FP8X4 = mybir.dt.float8_e4m3fn_x4
+FP4X4 = mybir.dt.float4_e2m1fn_x4
+ACT = mybir.ActivationFunctionType
+MULT = mybir.AluOpType.mult
+
+P = 128
+G = M // 512
+PASSES = R // 512
+NC = 128
+CH = B // NC
+
+
+def tile_bcs_gap_step_s13_kernel(tc, phi, coef_bytes, coef_scale, energy, v_words, v_scales, out):
+    nc = tc.nc
+    with ExitStack() as ctx:
+        keep = ctx.enter_context(tc.tile_pool(name="keep", bufs=1))
+        stage = ctx.enter_context(tc.tile_pool(name="stage", bufs=3))
+        ps_x = ctx.enter_context(tc.psum_pool(name="ps_x", bufs=4))
+        ps_g = ctx.enter_context(tc.psum_pool(name="ps_g", bufs=4))
+
+        en = keep.tile([P, G, 4, B], BF16, name="en", align_bytes=64)
+        ph = keep.tile([P, G, 4, R], BF16, name="ph", align_bytes=64)
+        cb = keep.tile([P, PASSES, 4, B], U8, name="cb", align_bytes=64)
+        cs = keep.tile([P, PASSES, 4], F32, name="cs", align_bytes=64)
+        vw = keep.tile([P, G, 2 * M], U8, name="vw", align_bytes=64)
+        vs = keep.tile([P, G, M], U8, name="vs", align_bytes=64)
+
+        phi_v = phi.rearrange("(g p t) k -> g p t k", p=P, t=4)
+        en_v = energy.rearrange("(g p t) n -> g p t n", p=P, t=4)
+        cb_v = coef_bytes.rearrange("(g p t) n -> p g (t n)", p=P, t=4)
+        cs_v = coef_scale.rearrange("(g p t) o -> p g (t o)", p=P, t=4)
+        out_v = out.rearrange("(q i p) (c n) -> q c p i n", i=4, p=P, n=NC)
+
+        def load_en(g):
+            nc.sync.dma_start(out=en[:, g, :, :], in_=en_v[g])
+
+        def load_phi(g, t0, t1):
+            nc.sync.dma_start(out=ph[:, g, t0:t1, :], in_=phi_v[g][:, t0:t1, :])
+
+        def load_cb(k):
+            nc.sync.dma_start(out=cb[:, k, :, :].rearrange("p t n -> p (t n)"), in_=cb_v[:, k, :])
+
+        warm = keep.tile([P, 1], F32, name="warm")
+        nc.vector.memset(warm[:], 1.0)
+        nc.scalar.activation(out=warm[:], in_=warm[:], func=ACT.Abs_reciprocal_sqrt)
+        ident = keep.tile([P, P], F32, name="ident", align_bytes=64)
+        make_identity(nc, ident[:])
+        nc.gpsimd.memset(vs[:].rearrange("p g n -> p (g n)").bitcast(U32), 0)
+
+        nc.sync.dma_start(out=cs[:], in_=cs_v)
+        load_cb(0)
+        load_en(0)
+        load_cb(1)
+        load_phi(0, 0, 2)
+        load_en(1)
+        load_phi(0, 2, 4)
+        load_en(2)
+        load_phi(1, 0, 2)
+        load_en(3)
+        load_phi(1, 2, 4)
+        load_phi(2, 0, 2)
+        load_phi(2, 2, 4)
+        load_phi(3, 0, 2)
+        load_phi(3, 2, 4)
+        for quad in range(4):
+            nc.sync.dma_start(
+                out=vs[32 * quad : 32 * quad + 4, :, :].bitcast(I32),
+                in_=v_scales[:, 4 * quad : 4 * quad + 4, :].rearrange("g r n -> r g n").bitcast(I32),
+            )
+        for q in range(4):
+            nc.sync.dma_start(out=vw[:, :, 1024 * q : 1024 * (q + 1)], in_=v_words.rearrange("g p b -> p g b")[:, :, 1024 * q : 1024 * (q + 1)])
+
+        cc = keep.tile([P, PASSES, B], U32, name="cc", align_bytes=64)
+        csc = keep.tile([P, PASSES, B], U8, name="csc", align_bytes=64)
+        wide = keep.tile([P, PASSES, 4, B], BF16, name="wide", align_bytes=64)
+        cgrp = keep.tile([P, PASSES, B, 4], BF16, name="cgrp", align_bytes=64)
+        qr = keep.tile([P, G * 4, B], F32, name="qr", align_bytes=64)
+        pc = keep.tile([P, G * 4, PASSES, P], U32, name="pc", align_bytes=64)
+        psc = keep.tile([P, G * 4, PASSES, P], U8, name="psc", align_bytes=64)
+
+        def coef_widen(k, on_scalar):
+            for t in range(4):
+                if on_scalar:
+                    nc.scalar.activation(out=wide[:, k, t, :], in_=cb[:, k, t, :].bitcast(FP8), func=ACT.Copy, scale=cs[:, k, t : t + 1])
+                else:
+                    nc.vector.tensor_scalar(
+                        out=wide[:, k, t, :], in0=cb[:, k, t, :].bitcast(FP8), scalar1=cs[:, k, t : t + 1], scalar2=None, op0=MULT
+                    )
+
+        def coef_interleave(k):
+            nc.vector.tensor_copy(
+                out=cgrp[:, k, :, :].rearrange("p (c i) t -> p c t i", i=4),
+                in_=wide[:, k, :, :].rearrange("p t (c i) -> p c t i", i=4),
+            )
+
+        def coef_quant(k):
+            nc.vector.quantize_mx(
+                out=cc[:, k, :].bitcast(FP8X4), scales=csc[:, k, :], in_=cgrp[:, k, :, :].rearrange("p n t -> p (n t)")
+            )
+
+        def ars(g, a):
+            rows, cols = slice(4 * g, 4 * g + 4), slice(256 * a, 256 * a + 256)
+            nc.scalar.activation(out=qr[:, rows, cols], in_=en[:, g, :, cols], func=ACT.Abs_reciprocal_sqrt)
+
+        banks = {}
+        groups = {}
+
+        def transposes(j):
+            g, t = divmod(j, 4)
+            bank = ps_x.tile([P, PASSES, 2, P], F32, name="bank", tag="x")
+            words = ph[:, g, t, :].bitcast(F32)
+            for k in range(PASSES):
+                for u in range(2):
+                    nc.tensor.transpose(bank[:, k, u, :], words[:, 256 * k + u : 256 * (k + 1) : 2], ident[:])
+            banks[j] = bank
+
+        def evacuate(j, on_scalar):
+            grp = stage.tile([P, PASSES, P, 4], BF16, name="grp", tag="grp", bufs=6, align_bytes=64)
+            dst = grp[:].rearrange("p k r t -> p (k r t)").bitcast(F32).rearrange("p (k r u) -> p k r u", k=PASSES, u=2)
+            src = banks[j][:].rearrange("p k u r -> p k r u")
+            if on_scalar:
+                nc.scalar.copy(out=dst, in_=src)
+            else:
+                nc.vector.tensor_copy(out=dst, in_=src)
+            groups[j] = grp
+
+        def quant_phi(j):
+            nc.vector.quantize_mx(
+                out=pc[:, j, :, :].rearrange("p k r -> p (k r)").bitcast(FP8X4),
+                scales=psc[:, j, :, :].rearrange("p k r -> p (k r)"),
+                in_=groups[j][:].rearrange("p k r t -> p (k r t)"),
+            )
+
+        gbanks = {}
+
+        def mm1(g, c):
+            bank = ps_g.tile([P, 4, NC], F32, name="gbank", tag="g")
+            cols = slice(c * NC, (c + 1) * NC)
+            for t in range(4):
+                for k in range(PASSES):
+                    nc.tensor.matmul_mx(
+                        out=bank[:, t, :],
+                        lhsT=pc[:, 4 * g + t, k, :].bitcast(FP8X4),
+                        lhsT_scale=psc[:, 4 * g + t, k, :],
+                        rhs=cc[:, k, cols].bitcast(FP8X4),
+                        rhs_scale=csc[:, k, cols],
+                        start=(k == 0),
+                        stop=(k == PASSES - 1),
+                    )
+            gbanks[g, c] = bank
+
+        th = {}
+        hcodes = {}
+        hscales = {}
+        hgrp = {}
+
+        def square(g, c, on_scalar):
+            r = qr[:, 4 * g : 4 * g + 4, c * NC : (c + 1) * NC]
+            if on_scalar:
+                nc.scalar.activation(out=r, in_=r, func=ACT.Square)
+            else:
+                nc.vector.tensor_tensor(out=r, in0=r, in1=r, op=MULT)
+
+        def tanh(g, c):
+            if c not in th:
+                th[c] = stage.tile([P, G * 4, NC], F32, name="th", tag="th", bufs=3, align_bytes=64)
+            nc.scalar.activation(out=th[c][:, 4 * g : 4 * g + 4, :], in_=en[:, g, :, c * NC : (c + 1) * NC], func=ACT.Tanh)
+
+        def weights_mult(g, c):
+            rows = slice(4 * g, 4 * g + 4)
+            cols = slice(c * NC, (c + 1) * NC)
+            nc.vector.tensor_tensor(out=th[c][:, rows, :], in0=th[c][:, rows, :], in1=qr[:, rows, cols], op=MULT)
+
+        def make_h(g, c):
+            hg = stage.tile([P, NC, 4], BF16, name="hg", tag="hg", bufs=4, align_bytes=64)
+            nc.vector.tensor_tensor(
+                out=hg[:].rearrange("p (c i) t -> p c t i", i=4),
+                in0=gbanks[g, c][:].rearrange("p t (c i) -> p c t i", i=4),
+                in1=th[c][:, 4 * g : 4 * g + 4, :].rearrange("p t (c i) -> p c t i", i=4),
+                op=MULT,
+            )
+            hgrp[g, c] = hg
+
+        def quant_h(g, c):
+            if c not in hcodes:
+                hcodes[c] = stage.tile([P, G, NC], U32, name="hc", tag="hc", bufs=3, align_bytes=64)
+                hscales[c] = stage.tile([P, G, NC], U8, name="hs", tag="hs", bufs=3, align_bytes=64)
+            nc.vector.quantize_mx(
+                out=hcodes[c][:, g, :].bitcast(FP8X4),
+                scales=hscales[c][:, g, :],
+                in_=hgrp[g, c][:].rearrange("p n t -> p (n t)"),
+            )
+
+        obanks = {}
+
+        def mm2(q, c):
+            bank = ps_x.tile([P, 4, NC], F32, name="obank", tag="x")
+            for i in range(4):
+                tile_i = 4 * q + i
+                for g in range(G):
+                    nc.tensor.matmul_mx(
+                        out=bank[:, i, :],
+                        lhsT=vw[:, g, 256 * tile_i : 256 * (tile_i + 1)].bitcast(FP4X4),
+                        lhsT_scale=vs[:, g, P * tile_i : P * (tile_i + 1)],
+                        rhs=hcodes[c][:, g, :].bitcast(FP8X4),
+                        rhs_scale=hscales[c][:, g, :],
+                        start=(g == 0),
+                        stop=(g == G - 1),
+                    )
+            obanks[q, c] = bank
+
+        def store(q, c, on_scalar):
+            o = stage.tile([P, 4, NC], F32, name="o", tag="o", bufs=4, align_bytes=64)
+            if on_scalar:
+                nc.scalar.copy(out=o[:], in_=obanks[q, c][:])
+            else:
+                nc.vector.tensor_copy(out=o[:], in_=obanks[q, c][:])
+            nc.sync.dma_start(out=out_v[q, c], in_=o[:])
+
+        with tc.manual_schedule():
+            coef_widen(0, True)
+            ars(0, 0)
+            coef_interleave(0)
+            coef_widen(1, True)
+            square(0, 0, False)
+            transposes(1)
+            coef_quant(0)
+            transposes(0)
+            square(0, 1, True)
+            coef_interleave(1)
+            ars(1, 0)
+            transposes(3)
+            evacuate(1, True)
+            evacuate(0, False)
+            transposes(2)
+            square(1, 0, True)
+            coef_quant(1)
+            ars(2, 0)
+            quant_phi(1)
+            quant_phi(0)
+            evacuate(3, False)
+            transposes(5)
+            evacuate(2, True)
+            square(1, 1, False)
+            transposes(4)
+            square(2, 0, True)
+            quant_phi(3)
+            quant_phi(2)
+            ars(3, 0)
+            evacuate(5, False)
+            mm1(0, 0)
+            evacuate(4, False)
+            square(2, 1, True)
+            transposes(7)
+            quant_phi(5)
+            quant_phi(4)
+            tanh(0, 0)
+            transposes(6)
+            square(3, 0, False)
+            transposes(9)
+            evacuate(7, False)
+            transposes(8)
+            evacuate(9, False)
+            transposes(11)
+            quant_phi(7)
+            evacuate(8, True)
+            transposes(10)
+            quant_phi(9)
+            weights_mult(0, 0)
+            mm1(0, 1)
+            evacuate(11, True)
+            quant_phi(8)
+            evacuate(10, True)
+            evacuate(6, False)
+            transposes(13)
+            tanh(1, 0)
+            quant_phi(11)
+            transposes(15)
+            quant_phi(10)
+            evacuate(13, True)
+            quant_phi(6)
+            transposes(14)
+            weights_mult(1, 0)
+            evacuate(15, True)
+            transposes(12)
+            quant_phi(13)
+            evacuate(14, True)
+            mm1(1, 0)
+            make_h(0, 0)
+            evacuate(12, True)
+            quant_phi(15)
+            mm1(2, 0)
+            quant_phi(14)
+            tanh(2, 0)
+            quant_phi(12)
+            mm1(2, 1)
+            quant_h(0, 0)
+            tanh(3, 0)
+            make_h(1, 0)
+            tanh(3, 1)
+            weights_mult(2, 0)
+            mm1(3, 0)
+            tanh(2, 1)
+            weights_mult(3, 0)
+            tanh(1, 1)
+            quant_h(1, 0)
+            make_h(2, 0)
+            tanh(0, 1)
+            make_h(3, 0)
+            mm1(3, 1)
+            square(3, 1, True)
+            quant_h(2, 0)
+            mm1(1, 1)
+            weights_mult(2, 1)
+            ars(3, 1)
+            quant_h(3, 0)
+            weights_mult(3, 1)
+            mm2(0, 0)
+            make_h(2, 1)
+            make_h(3, 1)
+            mm2(1, 0)
+            quant_h(2, 1)
+            weights_mult(1, 1)
+            ars(2, 1)
+            quant_h(3, 1)
+            square(3, 2, False)
+            mm2(2, 0)
+            make_h(1, 1)
+            ars(1, 1)
+            square(2, 2, False)
+            mm2(3, 0)
+            quant_h(1, 1)
+            square(3, 3, True)
+            weights_mult(0, 1)
+            square(1, 2, True)
+            square(2, 3, False)
+            ars(0, 1)
+            mm1(3, 2)
+            make_h(0, 1)
+            square(1, 3, False)
+            mm1(2, 2)
+            store(0, 0, True)
+            quant_h(0, 1)
+            mm1(1, 2)
+            square(0, 2, False)
+            tanh(3, 2)
+            square(0, 3, False)
+            mm1(0, 2)
+            store(1, 0, False)
+            mm2(3, 1)
+            store(2, 0, False)
+            store(3, 0, False)
+            tanh(2, 2)
+            mm2(2, 1)
+            weights_mult(3, 2)
+            tanh(1, 2)
+            weights_mult(2, 2)
+            tanh(0, 2)
+            mm2(1, 1)
+            weights_mult(1, 2)
+            tanh(3, 3)
+            make_h(3, 2)
+            store(3, 1, True)
+            weights_mult(0, 2)
+            mm1(3, 3)
+            tanh(2, 3)
+            quant_h(3, 2)
+            make_h(2, 2)
+            store(2, 1, True)
+            mm2(0, 1)
+            make_h(1, 2)
+            tanh(1, 3)
+            quant_h(2, 2)
+            store(1, 1, True)
+            make_h(0, 2)
+            mm1(2, 3)
+            tanh(0, 3)
+            quant_h(1, 2)
+            weights_mult(3, 3)
+            mm1(1, 3)
+            store(0, 1, True)
+            quant_h(0, 2)
+            mm1(0, 3)
+            weights_mult(2, 3)
+            make_h(3, 3)
+            mm2(3, 2)
+            make_h(2, 3)
+            quant_h(3, 3)
+            weights_mult(1, 3)
+            mm2(2, 2)
+            store(3, 2, True)
+            quant_h(2, 3)
+            weights_mult(0, 3)
+            make_h(1, 3)
+            mm2(1, 2)
+            store(2, 2, True)
+            make_h(0, 3)
+            quant_h(1, 3)
+            quant_h(0, 3)
+            mm2(0, 2)
+            store(1, 2, True)
+            mm2(3, 3)
+            store(0, 2, True)
+            mm2(2, 3)
+            store(3, 3, True)
+            mm2(1, 3)
+            store(2, 3, True)
+            mm2(0, 3)
+            store(1, 3, True)
+            store(0, 3, True)

@@ -29,8 +29,7 @@ def tile_bcs_gap_step_s13_kernel(tc, phi, coef_bytes, coef_scale, energy, v_word
     with ExitStack() as ctx:
         keep = ctx.enter_context(tc.tile_pool(name="keep", bufs=1))
         stage = ctx.enter_context(tc.tile_pool(name="stage", bufs=3))
-        ps_x = ctx.enter_context(tc.psum_pool(name="ps_x", bufs=4))
-        ps_g = ctx.enter_context(tc.psum_pool(name="ps_g", bufs=4))
+        ps_x = ctx.enter_context(tc.psum_pool(name="ps_x", bufs=8))
 
         en = keep.tile([P, G, 4, B], BF16, name="en", align_bytes=64)
         ph = keep.tile([P, G, 4, R], BF16, name="ph", align_bytes=64)
@@ -63,11 +62,11 @@ def tile_bcs_gap_step_s13_kernel(tc, phi, coef_bytes, coef_scale, energy, v_word
 
         nc.sync.dma_start(out=cs[:], in_=cs_v)
         load_cb(0)
-        load_en(0)
         load_cb(1)
+        load_en(0)
         load_phi(0, 0, 2)
-        load_en(1)
         load_phi(0, 2, 4)
+        load_en(1)
         load_en(2)
         load_phi(1, 0, 2)
         load_en(3)
@@ -81,8 +80,8 @@ def tile_bcs_gap_step_s13_kernel(tc, phi, coef_bytes, coef_scale, energy, v_word
                 out=vs[32 * quad : 32 * quad + 4, :, :].bitcast(I32),
                 in_=v_scales[:, 4 * quad : 4 * quad + 4, :].rearrange("g r n -> r g n").bitcast(I32),
             )
-        for q in range(4):
-            nc.sync.dma_start(out=vw[:, :, 1024 * q : 1024 * (q + 1)], in_=v_words.rearrange("g p b -> p g b")[:, :, 1024 * q : 1024 * (q + 1)])
+        for g in range(G):
+            nc.sync.dma_start(out=vw[:, g, :], in_=v_words[g])
 
         cc = keep.tile([P, PASSES, B], U32, name="cc", align_bytes=64)
         csc = keep.tile([P, PASSES, B], U8, name="csc", align_bytes=64)
@@ -112,9 +111,17 @@ def tile_bcs_gap_step_s13_kernel(tc, phi, coef_bytes, coef_scale, energy, v_word
                 out=cc[:, k, :].bitcast(FP8X4), scales=csc[:, k, :], in_=cgrp[:, k, :, :].rearrange("p n t -> p (n t)")
             )
 
+        split = 2 * NC
+
         def ars(g, a):
-            rows, cols = slice(4 * g, 4 * g + 4), slice(256 * a, 256 * a + 256)
-            nc.scalar.activation(out=qr[:, rows, cols], in_=en[:, g, :, cols], func=ACT.Abs_reciprocal_sqrt)
+            if a == 0:
+                nc.scalar.activation(out=qr[:, 4 * g : 4 * g + 4, :split], in_=en[:, g, :, :split], func=ACT.Abs_reciprocal_sqrt)
+            else:
+                nc.scalar.activation(
+                    out=qr[:, 8 * g : 8 * g + 8, split:],
+                    in_=en[:, 2 * g : 2 * g + 2, :, split:].rearrange("p g t n -> p (g t) n"),
+                    func=ACT.Abs_reciprocal_sqrt,
+                )
 
         banks = {}
         groups = {}
@@ -148,7 +155,7 @@ def tile_bcs_gap_step_s13_kernel(tc, phi, coef_bytes, coef_scale, energy, v_word
         gbanks = {}
 
         def mm1(g, c):
-            bank = ps_g.tile([P, 4, NC], F32, name="gbank", tag="g")
+            bank = ps_x.tile([P, 4, NC], F32, name="gbank", tag="x")
             cols = slice(c * NC, (c + 1) * NC)
             for t in range(4):
                 for k in range(PASSES):
@@ -180,10 +187,11 @@ def tile_bcs_gap_step_s13_kernel(tc, phi, coef_bytes, coef_scale, energy, v_word
                 th[c] = stage.tile([P, G * 4, NC], F32, name="th", tag="th", bufs=3, align_bytes=64)
             nc.scalar.activation(out=th[c][:, 4 * g : 4 * g + 4, :], in_=en[:, g, :, c * NC : (c + 1) * NC], func=ACT.Tanh)
 
-        def weights_mult(g, c):
+        def weights_mult(g, c, on_gpsimd=False):
             rows = slice(4 * g, 4 * g + 4)
             cols = slice(c * NC, (c + 1) * NC)
-            nc.vector.tensor_tensor(out=th[c][:, rows, :], in0=th[c][:, rows, :], in1=qr[:, rows, cols], op=MULT)
+            eng = nc.gpsimd if on_gpsimd else nc.vector
+            eng.tensor_tensor(out=th[c][:, rows, :], in0=th[c][:, rows, :], in1=qr[:, rows, cols], op=MULT)
 
         def make_h(g, c):
             hg = stage.tile([P, NC, 4], BF16, name="hg", tag="hg", bufs=4, align_bytes=64)
@@ -233,192 +241,190 @@ def tile_bcs_gap_step_s13_kernel(tc, phi, coef_bytes, coef_scale, energy, v_word
 
         with tc.manual_schedule():
             coef_widen(0, True)
-            ars(0, 0)
-            coef_interleave(0)
-            coef_widen(1, True)
-            square(0, 0, False)
-            transposes(1)
-            coef_quant(0)
-            transposes(0)
-            square(0, 1, True)
+            coef_widen(1, False)
             coef_interleave(1)
-            ars(1, 0)
+            ars(0, 0)
+            transposes(0)
+            transposes(1)
+            coef_interleave(0)
+            evacuate(0, True)
             transposes(3)
-            evacuate(1, True)
-            evacuate(0, False)
+            square(0, 0, True)
             transposes(2)
-            square(1, 0, True)
-            coef_quant(1)
-            ars(2, 0)
-            quant_phi(1)
+            evacuate(3, True)
             quant_phi(0)
-            evacuate(3, False)
-            transposes(5)
-            evacuate(2, True)
-            square(1, 1, False)
-            transposes(4)
-            square(2, 0, True)
-            quant_phi(3)
+            evacuate(1, False)
+            ars(1, 0)
+            evacuate(2, False)
+            quant_phi(1)
+            ars(2, 0)
             quant_phi(2)
+            quant_phi(3)
+            coef_quant(0)
+            transposes(5)
+            square(1, 0, True)
+            square(2, 0, False)
+            transposes(4)
+            evacuate(5, True)
+            coef_quant(1)
             ars(3, 0)
-            evacuate(5, False)
+            quant_phi(5)
             mm1(0, 0)
             evacuate(4, False)
-            square(2, 1, True)
-            transposes(7)
-            quant_phi(5)
-            quant_phi(4)
-            tanh(0, 0)
+            square(0, 1, True)
+            square(2, 1, False)
             transposes(6)
-            square(3, 0, False)
+            tanh(0, 0)
+            quant_phi(4)
+            transposes(7)
+            evacuate(6, False)
             transposes(9)
             evacuate(7, False)
             transposes(8)
-            evacuate(9, False)
-            transposes(11)
+            quant_phi(6)
+            transposes(10)
             quant_phi(7)
             evacuate(8, True)
-            transposes(10)
-            quant_phi(9)
-            weights_mult(0, 0)
-            mm1(0, 1)
-            evacuate(11, True)
-            quant_phi(8)
-            evacuate(10, True)
-            evacuate(6, False)
-            transposes(13)
+            evacuate(9, False)
+            transposes(11)
             tanh(1, 0)
-            quant_phi(11)
-            transposes(15)
-            quant_phi(10)
-            evacuate(13, True)
-            quant_phi(6)
+            weights_mult(0, 0, False)
+            mm1(1, 0)
+            evacuate(10, True)
+            quant_phi(8)
             transposes(14)
-            weights_mult(1, 0)
+            weights_mult(1, 0, False)
+            square(3, 0, True)
+            make_h(0, 0)
+            mm1(0, 2)
+            tanh(2, 0)
+            make_h(1, 0)
+            transposes(15)
+            evacuate(11, True)
+            weights_mult(2, 0, False)
+            tanh(0, 1)
+            transposes(13)
+            quant_phi(11)
             evacuate(15, True)
             transposes(12)
-            quant_phi(13)
-            evacuate(14, True)
-            mm1(1, 0)
-            make_h(0, 0)
-            evacuate(12, True)
-            quant_phi(15)
-            mm1(2, 0)
-            quant_phi(14)
-            tanh(2, 0)
-            quant_phi(12)
-            mm1(2, 1)
             quant_h(0, 0)
+            weights_mult(0, 1, False)
+            mm1(1, 2)
+            evacuate(13, True)
+            quant_phi(10)
+            evacuate(12, True)
+            quant_phi(9)
+            mm1(1, 1)
+            quant_phi(15)
             tanh(3, 0)
-            make_h(1, 0)
-            tanh(3, 1)
-            weights_mult(2, 0)
-            mm1(3, 0)
-            tanh(2, 1)
-            weights_mult(3, 0)
+            quant_phi(13)
+            mm1(2, 0)
+            quant_phi(12)
             tanh(1, 1)
             quant_h(1, 0)
+            mm1(2, 2)
+            weights_mult(3, 0, False)
+            evacuate(14, True)
+            mm1(0, 1)
             make_h(2, 0)
-            tanh(0, 1)
+            tanh(3, 1)
+            quant_phi(14)
+            mm1(2, 1)
+            tanh(2, 1)
+            quant_h(2, 0)
+            make_h(0, 1)
+            mm1(3, 0)
+            square(1, 1, True)
+            weights_mult(2, 1, False)
+            mm1(3, 2)
+            ars(1, 1)
             make_h(3, 0)
             mm1(3, 1)
-            square(3, 1, True)
-            quant_h(2, 0)
-            mm1(1, 1)
-            weights_mult(2, 1)
-            ars(3, 1)
+            quant_h(0, 1)
+            weights_mult(1, 1, False)
+            mm1(2, 3)
             quant_h(3, 0)
-            weights_mult(3, 1)
-            mm2(0, 0)
             make_h(2, 1)
-            make_h(3, 1)
+            make_h(1, 1)
             mm2(1, 0)
             quant_h(2, 1)
-            weights_mult(1, 1)
-            ars(2, 1)
-            quant_h(3, 1)
-            square(3, 2, False)
-            mm2(2, 0)
-            make_h(1, 1)
-            ars(1, 1)
-            square(2, 2, False)
-            mm2(3, 0)
+            square(3, 1, False)
             quant_h(1, 1)
-            square(3, 3, True)
-            weights_mult(0, 1)
-            square(1, 2, True)
-            square(2, 3, False)
             ars(0, 1)
-            mm1(3, 2)
-            make_h(0, 1)
-            square(1, 3, False)
-            mm1(2, 2)
-            store(0, 0, True)
-            quant_h(0, 1)
-            mm1(1, 2)
-            square(0, 2, False)
-            tanh(3, 2)
-            square(0, 3, False)
-            mm1(0, 2)
+            mm2(0, 0)
+            weights_mult(3, 1, False)
             store(1, 0, False)
-            mm2(3, 1)
-            store(2, 0, False)
-            store(3, 0, False)
-            tanh(2, 2)
-            mm2(2, 1)
-            weights_mult(3, 2)
-            tanh(1, 2)
-            weights_mult(2, 2)
+            make_h(3, 1)
+            mm2(2, 0)
+            store(0, 0, False)
+            square(3, 2, True)
+            quant_h(3, 1)
+            square(1, 2, False)
+            mm2(3, 0)
             tanh(0, 2)
-            mm2(1, 1)
-            weights_mult(1, 2)
-            tanh(3, 3)
-            make_h(3, 2)
+            store(2, 0, False)
+            square(0, 2, False)
+            mm2(0, 1)
+            square(2, 2, False)
+            store(3, 0, False)
+            tanh(1, 2)
+            weights_mult(0, 2, False)
+            mm2(3, 1)
+            tanh(2, 2)
+            weights_mult(1, 2, False)
+            tanh(3, 2)
+            weights_mult(2, 2, False)
+            store(0, 1, True)
+            mm2(2, 1)
+            weights_mult(3, 2, False)
             store(3, 1, True)
-            weights_mult(0, 2)
-            mm1(3, 3)
-            tanh(2, 3)
-            quant_h(3, 2)
+            make_h(1, 2)
+            square(3, 3, True)
+            mm1(0, 3)
             make_h(2, 2)
             store(2, 1, True)
-            mm2(0, 1)
-            make_h(1, 2)
-            tanh(1, 3)
-            quant_h(2, 2)
-            store(1, 1, True)
-            make_h(0, 2)
-            mm1(2, 3)
-            tanh(0, 3)
+            mm2(1, 1)
             quant_h(1, 2)
-            weights_mult(3, 3)
+            tanh(0, 3)
+            make_h(0, 2)
+            square(0, 3, True)
+            quant_h(2, 2)
+            make_h(3, 2)
             mm1(1, 3)
-            store(0, 1, True)
+            tanh(1, 3)
             quant_h(0, 2)
-            mm1(0, 3)
-            weights_mult(2, 3)
-            make_h(3, 3)
-            mm2(3, 2)
-            make_h(2, 3)
-            quant_h(3, 3)
-            weights_mult(1, 3)
-            mm2(2, 2)
-            store(3, 2, True)
-            quant_h(2, 3)
-            weights_mult(0, 3)
-            make_h(1, 3)
+            store(1, 1, False)
+            square(1, 3, True)
+            mm1(3, 3)
+            quant_h(3, 2)
+            square(2, 3, True)
+            weights_mult(0, 3, False)
             mm2(1, 2)
-            store(2, 2, True)
+            tanh(3, 3)
+            weights_mult(1, 3, False)
+            tanh(2, 3)
             make_h(0, 3)
-            quant_h(1, 3)
-            quant_h(0, 3)
             mm2(0, 2)
+            weights_mult(3, 3, False)
             store(1, 2, True)
-            mm2(3, 3)
+            weights_mult(2, 3, False)
+            make_h(3, 3)
+            mm2(2, 2)
             store(0, 2, True)
-            mm2(2, 3)
-            store(3, 3, True)
+            make_h(2, 3)
+            make_h(1, 3)
+            mm2(3, 2)
+            store(2, 2, True)
+            quant_h(0, 3)
+            quant_h(2, 3)
+            quant_h(1, 3)
+            quant_h(3, 3)
             mm2(1, 3)
-            store(2, 3, True)
-            mm2(0, 3)
+            store(3, 2, True)
+            mm2(3, 3)
             store(1, 3, True)
+            mm2(0, 3)
+            store(3, 3, True)
+            mm2(2, 3)
             store(0, 3, True)
+            store(2, 3, True)

@@ -62,15 +62,15 @@ def tile_bcs_gap_step_s13_kernel(tc, phi, coef_bytes, coef_scale, energy, v_word
 
         nc.sync.dma_start(out=cs[:], in_=cs_v)
         load_cb(0)
-        load_cb(1)
         load_en(0)
+        load_cb(1)
         load_phi(0, 0, 2)
         load_phi(0, 2, 4)
         load_en(1)
-        load_en(2)
         load_phi(1, 0, 2)
-        load_en(3)
+        load_en(2)
         load_phi(1, 2, 4)
+        load_en(3)
         load_phi(2, 0, 2)
         load_phi(2, 2, 4)
         load_phi(3, 0, 2)
@@ -242,189 +242,189 @@ def tile_bcs_gap_step_s13_kernel(tc, phi, coef_bytes, coef_scale, energy, v_word
         with tc.manual_schedule():
             coef_widen(0, True)
             coef_widen(1, False)
-            coef_interleave(1)
             ars(0, 0)
             transposes(0)
-            transposes(1)
             coef_interleave(0)
+            transposes(1)
             evacuate(0, True)
-            transposes(3)
-            square(0, 0, True)
             transposes(2)
-            evacuate(3, True)
-            quant_phi(0)
-            evacuate(1, False)
+            evacuate(1, True)
+            coef_interleave(1)
+            transposes(3)
+            evacuate(2, True)
             ars(1, 0)
-            evacuate(2, False)
-            quant_phi(1)
-            ars(2, 0)
-            quant_phi(2)
-            quant_phi(3)
-            coef_quant(0)
-            transposes(5)
-            square(1, 0, True)
-            square(2, 0, False)
+            evacuate(3, False)
             transposes(4)
-            evacuate(5, True)
             coef_quant(1)
-            ars(3, 0)
-            quant_phi(5)
-            mm1(0, 0)
-            evacuate(4, False)
-            square(0, 1, True)
-            square(2, 1, False)
+            square(0, 0, True)
+            transposes(5)
+            quant_phi(2)
+            evacuate(4, True)
+            coef_quant(0)
+            ars(2, 0)
+            quant_phi(1)
+            quant_phi(0)
             transposes(6)
-            tanh(0, 0)
+            quant_phi(3)
+            evacuate(5, True)
             quant_phi(4)
             transposes(7)
+            square(2, 0, False)
+            square(1, 0, True)
+            mm1(0, 1)
+            quant_phi(5)
+            ars(3, 0)
+            evacuate(7, False)
+            mm1(0, 0)
             evacuate(6, False)
             transposes(9)
-            evacuate(7, False)
-            transposes(8)
-            quant_phi(6)
-            transposes(10)
+            square(1, 1, True)
             quant_phi(7)
-            evacuate(8, True)
+            quant_phi(6)
+            tanh(0, 0)
+            transposes(8)
             evacuate(9, False)
+            transposes(10)
+            evacuate(8, False)
             transposes(11)
-            tanh(1, 0)
-            weights_mult(0, 0, False)
-            mm1(1, 0)
-            evacuate(10, True)
-            quant_phi(8)
-            transposes(14)
-            weights_mult(1, 0, False)
-            square(3, 0, True)
-            make_h(0, 0)
-            mm1(0, 2)
-            tanh(2, 0)
-            make_h(1, 0)
-            transposes(15)
-            evacuate(11, True)
-            weights_mult(2, 0, False)
-            tanh(0, 1)
-            transposes(13)
-            quant_phi(11)
-            evacuate(15, True)
-            transposes(12)
-            quant_h(0, 0)
-            weights_mult(0, 1, False)
-            mm1(1, 2)
-            evacuate(13, True)
-            quant_phi(10)
-            evacuate(12, True)
             quant_phi(9)
-            mm1(1, 1)
-            quant_phi(15)
+            transposes(12)
+            quant_phi(8)
+            evacuate(11, False)
+            transposes(13)
+            evacuate(10, True)
+            weights_mult(0, 0, True)
+            evacuate(12, False)
+            transposes(15)
+            square(3, 0, True)
+            evacuate(13, False)
+            transposes(14)
             tanh(3, 0)
-            quant_phi(13)
-            mm1(2, 0)
+            mm1(1, 0)
             quant_phi(12)
-            tanh(1, 1)
-            quant_h(1, 0)
-            mm1(2, 2)
-            weights_mult(3, 0, False)
+            evacuate(15, True)
+            quant_phi(10)
+            make_h(0, 0)
+            weights_mult(3, 0, True)
             evacuate(14, True)
-            mm1(0, 1)
-            make_h(2, 0)
-            tanh(3, 1)
+            mm1(1, 1)
+            tanh(1, 0)
+            mm1(1, 2)
+            quant_h(0, 0)
+            tanh(2, 0)
+            mm1(0, 2)
+            quant_phi(15)
+            quant_phi(13)
+            tanh(0, 1)
+            mm1(1, 3)
+            quant_phi(11)
             quant_phi(14)
+            tanh(1, 1)
+            mm1(2, 0)
+            weights_mult(1, 0, False)
+            tanh(3, 1)
+            weights_mult(2, 0, False)
+            mm1(3, 0)
+            square(2, 1, True)
+            make_h(1, 0)
+            weights_mult(1, 1, True)
+            square(0, 1, True)
+            make_h(2, 0)
+            mm1(3, 1)
+            square(3, 1, True)
+            make_h(3, 0)
+            weights_mult(0, 1, True)
             mm1(2, 1)
             tanh(2, 1)
+            make_h(1, 1)
+            mm1(2, 2)
+            ars(0, 1)
+            quant_h(3, 0)
+            quant_h(1, 0)
+            mm1(3, 2)
             quant_h(2, 0)
             make_h(0, 1)
-            mm1(3, 0)
-            square(1, 1, True)
-            weights_mult(2, 1, False)
-            mm1(3, 2)
-            ars(1, 1)
-            make_h(3, 0)
-            mm1(3, 1)
-            quant_h(0, 1)
-            weights_mult(1, 1, False)
-            mm1(2, 3)
-            quant_h(3, 0)
-            make_h(2, 1)
-            make_h(1, 1)
-            mm2(1, 0)
-            quant_h(2, 1)
-            square(3, 1, False)
-            quant_h(1, 1)
-            ars(0, 1)
-            mm2(0, 0)
-            weights_mult(3, 1, False)
-            store(1, 0, False)
-            make_h(3, 1)
+            weights_mult(2, 1, True)
             mm2(2, 0)
-            store(0, 0, False)
-            square(3, 2, True)
-            quant_h(3, 1)
-            square(1, 2, False)
-            mm2(3, 0)
-            tanh(0, 2)
+            quant_h(0, 1)
+            quant_h(1, 1)
+            make_h(2, 1)
+            weights_mult(3, 1, True)
             store(2, 0, False)
+            mm2(3, 0)
+            quant_h(2, 1)
+            make_h(3, 1)
+            ars(1, 1)
             square(0, 2, False)
-            mm2(0, 1)
-            square(2, 2, False)
+            mm2(0, 0)
+            square(1, 2, False)
+            quant_h(3, 1)
             store(3, 0, False)
+            mm2(1, 0)
+            store(0, 0, True)
+            square(3, 2, False)
             tanh(1, 2)
+            square(2, 2, False)
+            mm2(2, 1)
+            store(1, 0, False)
+            square(2, 3, False)
+            mm2(1, 1)
+            square(1, 3, False)
+            tanh(0, 2)
+            weights_mult(1, 2, False)
+            tanh(3, 2)
             weights_mult(0, 2, False)
             mm2(3, 1)
             tanh(2, 2)
-            weights_mult(1, 2, False)
-            tanh(3, 2)
-            weights_mult(2, 2, False)
-            store(0, 1, True)
-            mm2(2, 1)
-            weights_mult(3, 2, False)
-            store(3, 1, True)
             make_h(1, 2)
+            weights_mult(3, 2, True)
+            store(1, 1, True)
+            make_h(0, 2)
+            store(2, 1, True)
+            mm2(0, 1)
+            store(3, 1, False)
+            weights_mult(2, 2, True)
+            square(0, 3, True)
+            make_h(3, 2)
             square(3, 3, True)
             mm1(0, 3)
-            make_h(2, 2)
-            store(2, 1, True)
-            mm2(1, 1)
-            quant_h(1, 2)
-            tanh(0, 3)
-            make_h(0, 2)
-            square(0, 3, True)
-            quant_h(2, 2)
-            make_h(3, 2)
-            mm1(1, 3)
-            tanh(1, 3)
             quant_h(0, 2)
-            store(1, 1, False)
-            square(1, 3, True)
-            mm1(3, 3)
+            store(0, 1, True)
+            quant_h(1, 2)
+            make_h(2, 2)
+            mm1(2, 3)
+            tanh(0, 3)
             quant_h(3, 2)
-            square(2, 3, True)
-            weights_mult(0, 3, False)
-            mm2(1, 2)
-            tanh(3, 3)
-            weights_mult(1, 3, False)
+            mm1(3, 3)
+            quant_h(2, 2)
             tanh(2, 3)
-            make_h(0, 3)
+            weights_mult(0, 3, False)
             mm2(0, 2)
-            weights_mult(3, 3, False)
-            store(1, 2, True)
+            tanh(3, 3)
             weights_mult(2, 3, False)
-            make_h(3, 3)
-            mm2(2, 2)
-            store(0, 2, True)
+            tanh(1, 3)
+            make_h(0, 3)
+            weights_mult(3, 3, True)
+            mm2(1, 2)
             make_h(2, 3)
-            make_h(1, 3)
-            mm2(3, 2)
-            store(2, 2, True)
+            store(0, 2, True)
             quant_h(0, 3)
             quant_h(2, 3)
-            quant_h(1, 3)
+            make_h(3, 3)
+            weights_mult(1, 3, True)
+            mm2(3, 2)
+            store(1, 2, True)
             quant_h(3, 3)
-            mm2(1, 3)
+            make_h(1, 3)
+            mm2(2, 2)
             store(3, 2, True)
+            quant_h(1, 3)
+            mm2(0, 3)
+            store(2, 2, True)
+            mm2(1, 3)
+            store(0, 3, True)
             mm2(3, 3)
             store(1, 3, True)
-            mm2(0, 3)
-            store(3, 3, True)
             mm2(2, 3)
-            store(0, 3, True)
+            store(3, 3, True)
             store(2, 3, True)

from contextlib import ExitStack

import concourse.mybir as mybir
from concourse.masks import make_identity

M, R, B = 2048, 1024, 512
FLOPS = 2 * M * R * B + 2 * M * M * B

F32 = mybir.dt.float32
BF16 = mybir.dt.bfloat16
U32 = mybir.dt.uint32
I32 = mybir.dt.int32
U8 = mybir.dt.uint8
FP8 = mybir.dt.float8_e4m3fn
FP8X4 = mybir.dt.float8_e4m3fn_x4
FP4X4 = mybir.dt.float4_e2m1fn_x4
ACT = mybir.ActivationFunctionType
MULT = mybir.AluOpType.mult

P = 128
G = M // 512
PASSES = R // 512
NC = 128
CH = B // NC


def tile_bcs_gap_step_s13_kernel(tc, phi, coef_bytes, coef_scale, energy, v_words, v_scales, out):
    nc = tc.nc
    with ExitStack() as ctx:
        keep = ctx.enter_context(tc.tile_pool(name="keep", bufs=1))
        stage = ctx.enter_context(tc.tile_pool(name="stage", bufs=3))
        ps_x = ctx.enter_context(tc.psum_pool(name="ps_x", bufs=8))

        en = keep.tile([P, G, 4, B], BF16, name="en", align_bytes=64)
        ph = keep.tile([P, G, 4, R], BF16, name="ph", align_bytes=64)
        cb = keep.tile([P, PASSES, 4, B], U8, name="cb", align_bytes=64)
        cs = keep.tile([P, PASSES, 4], F32, name="cs", align_bytes=64)
        vw = keep.tile([P, G, 2 * M], U8, name="vw", align_bytes=64)
        vs = keep.tile([P, G, M], U8, name="vs", align_bytes=64)

        phi_v = phi.rearrange("(g p t) k -> g p t k", p=P, t=4)
        en_v = energy.rearrange("(g p t) n -> g p t n", p=P, t=4)
        cb_v = coef_bytes.rearrange("(g p t) n -> p g (t n)", p=P, t=4)
        cs_v = coef_scale.rearrange("(g p t) o -> p g (t o)", p=P, t=4)
        out_v = out.rearrange("(q i p) (c n) -> q c p i n", i=4, p=P, n=NC)

        def load_en(g):
            nc.sync.dma_start(out=en[:, g, :, :], in_=en_v[g])

        def load_phi(g, t0, t1):
            nc.sync.dma_start(out=ph[:, g, t0:t1, :], in_=phi_v[g][:, t0:t1, :])

        def load_cb(k):
            nc.sync.dma_start(out=cb[:, k, :, :].rearrange("p t n -> p (t n)"), in_=cb_v[:, k, :])

        warm = keep.tile([P, 1], F32, name="warm")
        nc.vector.memset(warm[:], 1.0)
        nc.scalar.activation(out=warm[:], in_=warm[:], func=ACT.Abs_reciprocal_sqrt)
        ident = keep.tile([P, P], F32, name="ident", align_bytes=64)
        make_identity(nc, ident[:])
        nc.gpsimd.memset(vs[:].rearrange("p g n -> p (g n)").bitcast(U32), 0)

        nc.sync.dma_start(out=cs[:], in_=cs_v)
        load_cb(0)
        load_en(0)
        load_cb(1)
        load_phi(0, 0, 2)
        load_phi(0, 2, 4)
        load_en(1)
        load_phi(1, 0, 2)
        load_en(2)
        load_phi(1, 2, 4)
        load_en(3)
        load_phi(2, 0, 2)
        load_phi(2, 2, 4)
        load_phi(3, 0, 2)
        load_phi(3, 2, 4)
        for quad in range(4):
            nc.sync.dma_start(
                out=vs[32 * quad : 32 * quad + 4, :, :].bitcast(I32),
                in_=v_scales[:, 4 * quad : 4 * quad + 4, :].rearrange("g r n -> r g n").bitcast(I32),
            )
        for g in range(G):
            nc.sync.dma_start(out=vw[:, g, :], in_=v_words[g])

        cc = keep.tile([P, PASSES, B], U32, name="cc", align_bytes=64)
        csc = keep.tile([P, PASSES, B], U8, name="csc", align_bytes=64)
        wide = keep.tile([P, PASSES, 4, B], BF16, name="wide", align_bytes=64)
        cgrp = keep.tile([P, PASSES, B, 4], BF16, name="cgrp", align_bytes=64)
        qr = keep.tile([P, G * 4, B], F32, name="qr", align_bytes=64)
        pc = keep.tile([P, G * 4, PASSES, P], U32, name="pc", align_bytes=64)
        psc = keep.tile([P, G * 4, PASSES, P], U8, name="psc", align_bytes=64)

        def coef_widen(k, on_scalar):
            for t in range(4):
                if on_scalar:
                    nc.scalar.activation(out=wide[:, k, t, :], in_=cb[:, k, t, :].bitcast(FP8), func=ACT.Copy, scale=cs[:, k, t : t + 1])
                else:
                    nc.vector.tensor_scalar(
                        out=wide[:, k, t, :], in0=cb[:, k, t, :].bitcast(FP8), scalar1=cs[:, k, t : t + 1], scalar2=None, op0=MULT
                    )

        def coef_interleave(k):
            nc.vector.tensor_copy(
                out=cgrp[:, k, :, :].rearrange("p (c i) t -> p c t i", i=4),
                in_=wide[:, k, :, :].rearrange("p t (c i) -> p c t i", i=4),
            )

        def coef_quant(k):
            nc.vector.quantize_mx(
                out=cc[:, k, :].bitcast(FP8X4), scales=csc[:, k, :], in_=cgrp[:, k, :, :].rearrange("p n t -> p (n t)")
            )

        split = 2 * NC

        def ars(g, a):
            if a == 0:
                nc.scalar.activation(out=qr[:, 4 * g : 4 * g + 4, :split], in_=en[:, g, :, :split], func=ACT.Abs_reciprocal_sqrt)
            else:
                nc.scalar.activation(
                    out=qr[:, 8 * g : 8 * g + 8, split:],
                    in_=en[:, 2 * g : 2 * g + 2, :, split:].rearrange("p g t n -> p (g t) n"),
                    func=ACT.Abs_reciprocal_sqrt,
                )

        banks = {}
        groups = {}

        def transposes(j):
            g, t = divmod(j, 4)
            bank = ps_x.tile([P, PASSES, 2, P], F32, name="bank", tag="x")
            words = ph[:, g, t, :].bitcast(F32)
            for k in range(PASSES):
                for u in range(2):
                    nc.tensor.transpose(bank[:, k, u, :], words[:, 256 * k + u : 256 * (k + 1) : 2], ident[:])
            banks[j] = bank

        def evacuate(j, on_scalar):
            grp = stage.tile([P, PASSES, P, 4], BF16, name="grp", tag="grp", bufs=6, align_bytes=64)
            dst = grp[:].rearrange("p k r t -> p (k r t)").bitcast(F32).rearrange("p (k r u) -> p k r u", k=PASSES, u=2)
            src = banks[j][:].rearrange("p k u r -> p k r u")
            if on_scalar:
                nc.scalar.copy(out=dst, in_=src)
            else:
                nc.vector.tensor_copy(out=dst, in_=src)
            groups[j] = grp

        def quant_phi(j):
            nc.vector.quantize_mx(
                out=pc[:, j, :, :].rearrange("p k r -> p (k r)").bitcast(FP8X4),
                scales=psc[:, j, :, :].rearrange("p k r -> p (k r)"),
                in_=groups[j][:].rearrange("p k r t -> p (k r t)"),
            )

        gbanks = {}

        def mm1(g, c):
            bank = ps_x.tile([P, 4, NC], F32, name="gbank", tag="x")
            cols = slice(c * NC, (c + 1) * NC)
            for t in range(4):
                for k in range(PASSES):
                    nc.tensor.matmul_mx(
                        out=bank[:, t, :],
                        lhsT=pc[:, 4 * g + t, k, :].bitcast(FP8X4),
                        lhsT_scale=psc[:, 4 * g + t, k, :],
                        rhs=cc[:, k, cols].bitcast(FP8X4),
                        rhs_scale=csc[:, k, cols],
                        start=(k == 0),
                        stop=(k == PASSES - 1),
                    )
            gbanks[g, c] = bank

        th = {}
        hcodes = {}
        hscales = {}
        hgrp = {}

        def square(g, c, on_scalar):
            r = qr[:, 4 * g : 4 * g + 4, c * NC : (c + 1) * NC]
            if on_scalar:
                nc.scalar.activation(out=r, in_=r, func=ACT.Square)
            else:
                nc.vector.tensor_tensor(out=r, in0=r, in1=r, op=MULT)

        def tanh(g, c):
            if c not in th:
                th[c] = stage.tile([P, G * 4, NC], F32, name="th", tag="th", bufs=3, align_bytes=64)
            nc.scalar.activation(out=th[c][:, 4 * g : 4 * g + 4, :], in_=en[:, g, :, c * NC : (c + 1) * NC], func=ACT.Tanh)

        def weights_mult(g, c, on_gpsimd=False):
            rows = slice(4 * g, 4 * g + 4)
            cols = slice(c * NC, (c + 1) * NC)
            eng = nc.gpsimd if on_gpsimd else nc.vector
            eng.tensor_tensor(out=th[c][:, rows, :], in0=th[c][:, rows, :], in1=qr[:, rows, cols], op=MULT)

        def make_h(g, c):
            hg = stage.tile([P, NC, 4], BF16, name="hg", tag="hg", bufs=4, align_bytes=64)
            nc.vector.tensor_tensor(
                out=hg[:].rearrange("p (c i) t -> p c t i", i=4),
                in0=gbanks[g, c][:].rearrange("p t (c i) -> p c t i", i=4),
                in1=th[c][:, 4 * g : 4 * g + 4, :].rearrange("p t (c i) -> p c t i", i=4),
                op=MULT,
            )
            hgrp[g, c] = hg

        def quant_h(g, c):
            if c not in hcodes:
                hcodes[c] = stage.tile([P, G, NC], U32, name="hc", tag="hc", bufs=3, align_bytes=64)
                hscales[c] = stage.tile([P, G, NC], U8, name="hs", tag="hs", bufs=3, align_bytes=64)
            nc.vector.quantize_mx(
                out=hcodes[c][:, g, :].bitcast(FP8X4),
                scales=hscales[c][:, g, :],
                in_=hgrp[g, c][:].rearrange("p n t -> p (n t)"),
            )

        obanks = {}

        def mm2(q, c):
            bank = ps_x.tile([P, 4, NC], F32, name="obank", tag="x")
            for i in range(4):
                tile_i = 4 * q + i
                for g in range(G):
                    nc.tensor.matmul_mx(
                        out=bank[:, i, :],
                        lhsT=vw[:, g, 256 * tile_i : 256 * (tile_i + 1)].bitcast(FP4X4),
                        lhsT_scale=vs[:, g, P * tile_i : P * (tile_i + 1)],
                        rhs=hcodes[c][:, g, :].bitcast(FP8X4),
                        rhs_scale=hscales[c][:, g, :],
                        start=(g == 0),
                        stop=(g == G - 1),
                    )
            obanks[q, c] = bank

        def store(q, c, on_scalar):
            o = stage.tile([P, 4, NC], F32, name="o", tag="o", bufs=4, align_bytes=64)
            if on_scalar:
                nc.scalar.copy(out=o[:], in_=obanks[q, c][:])
            else:
                nc.vector.tensor_copy(out=o[:], in_=obanks[q, c][:])
            nc.sync.dma_start(out=out_v[q, c], in_=o[:])

        with tc.manual_schedule():
            coef_widen(0, True)
            coef_widen(1, False)
            ars(0, 0)
            transposes(0)
            coef_interleave(0)
            transposes(1)
            evacuate(0, True)
            transposes(2)
            evacuate(1, True)
            coef_interleave(1)
            transposes(3)
            evacuate(2, True)
            ars(1, 0)
            evacuate(3, False)
            transposes(4)
            coef_quant(1)
            square(0, 0, True)
            transposes(5)
            quant_phi(2)
            evacuate(4, True)
            coef_quant(0)
            ars(2, 0)
            quant_phi(1)
            quant_phi(0)
            transposes(6)
            quant_phi(3)
            evacuate(5, True)
            quant_phi(4)
            transposes(7)
            square(2, 0, False)
            square(1, 0, True)
            mm1(0, 1)
            quant_phi(5)
            ars(3, 0)
            evacuate(7, False)
            mm1(0, 0)
            evacuate(6, False)
            transposes(9)
            square(1, 1, True)
            quant_phi(7)
            quant_phi(6)
            tanh(0, 0)
            transposes(8)
            evacuate(9, False)
            transposes(10)
            evacuate(8, False)
            transposes(11)
            quant_phi(9)
            transposes(12)
            quant_phi(8)
            evacuate(11, False)
            transposes(13)
            evacuate(10, True)
            weights_mult(0, 0, True)
            evacuate(12, False)
            transposes(15)
            square(3, 0, True)
            evacuate(13, False)
            transposes(14)
            tanh(3, 0)
            mm1(1, 0)
            quant_phi(12)
            evacuate(15, True)
            quant_phi(10)
            make_h(0, 0)
            weights_mult(3, 0, True)
            evacuate(14, True)
            mm1(1, 1)
            tanh(1, 0)
            mm1(1, 2)
            quant_h(0, 0)
            tanh(2, 0)
            mm1(0, 2)
            quant_phi(15)
            quant_phi(13)
            tanh(0, 1)
            mm1(1, 3)
            quant_phi(11)
            quant_phi(14)
            tanh(1, 1)
            mm1(2, 0)
            weights_mult(1, 0, False)
            tanh(3, 1)
            weights_mult(2, 0, False)
            mm1(3, 0)
            square(2, 1, True)
            make_h(1, 0)
            weights_mult(1, 1, True)
            square(0, 1, True)
            make_h(2, 0)
            mm1(3, 1)
            square(3, 1, True)
            make_h(3, 0)
            weights_mult(0, 1, True)
            mm1(2, 1)
            tanh(2, 1)
            make_h(1, 1)
            mm1(2, 2)
            ars(0, 1)
            quant_h(3, 0)
            quant_h(1, 0)
            mm1(3, 2)
            quant_h(2, 0)
            make_h(0, 1)
            weights_mult(2, 1, True)
            mm2(2, 0)
            quant_h(0, 1)
            quant_h(1, 1)
            make_h(2, 1)
            weights_mult(3, 1, True)
            store(2, 0, False)
            mm2(3, 0)
            quant_h(2, 1)
            make_h(3, 1)
            ars(1, 1)
            square(0, 2, False)
            mm2(0, 0)
            square(1, 2, False)
            quant_h(3, 1)
            store(3, 0, False)
            mm2(1, 0)
            store(0, 0, True)
            square(3, 2, False)
            tanh(1, 2)
            square(2, 2, False)
            mm2(2, 1)
            store(1, 0, False)
            square(2, 3, False)
            mm2(1, 1)
            square(1, 3, False)
            tanh(0, 2)
            weights_mult(1, 2, False)
            tanh(3, 2)
            weights_mult(0, 2, False)
            mm2(3, 1)
            tanh(2, 2)
            make_h(1, 2)
            weights_mult(3, 2, True)
            store(1, 1, True)
            make_h(0, 2)
            store(2, 1, True)
            mm2(0, 1)
            store(3, 1, False)
            weights_mult(2, 2, True)
            square(0, 3, True)
            make_h(3, 2)
            square(3, 3, True)
            mm1(0, 3)
            quant_h(0, 2)
            store(0, 1, True)
            quant_h(1, 2)
            make_h(2, 2)
            mm1(2, 3)
            tanh(0, 3)
            quant_h(3, 2)
            mm1(3, 3)
            quant_h(2, 2)
            tanh(2, 3)
            weights_mult(0, 3, False)
            mm2(0, 2)
            tanh(3, 3)
            weights_mult(2, 3, False)
            tanh(1, 3)
            make_h(0, 3)
            weights_mult(3, 3, True)
            mm2(1, 2)
            make_h(2, 3)
            store(0, 2, True)
            quant_h(0, 3)
            quant_h(2, 3)
            make_h(3, 3)
            weights_mult(1, 3, True)
            mm2(3, 2)
            store(1, 2, True)
            quant_h(3, 3)
            make_h(1, 3)
            mm2(2, 2)
            store(3, 2, True)
            quant_h(1, 3)
            mm2(0, 3)
            store(2, 2, True)
            mm2(1, 3)
            store(0, 3, True)
            mm2(3, 3)
            store(1, 3, True)
            mm2(2, 3)
            store(3, 3, True)
            store(2, 3, True)
